import numpy as np, ml_dtypes
CORES = [8,136,40,168]
N = 4
import mx_ref
NC, G, KO, SH = 128, 2, 1, 3
C = np.float32(0.047)
BF = ml_dtypes.bfloat16
def cut(t, i, w=512):
    return t[:, w * i:w * i + w]
def tile(rs):
    return np.stack(rs, axis=2).reshape(128, -1).astype(BF)
def layer(w, X):
    out = []
    for i in range(G):
        for t in range(len(X)):
            p = mx_ref.matmul(mx_ref.quantize(cut(w, len(X) * i + t)), X[t])
            z = p if t == 0 else z + p
        out.append(z)
    return out
def act(Z):
    return [np.maximum(s * z, 0) * C for z in Z for s in (1, -1)]
def inputs(rng, e, E):
    def f(*shape):
        v = (rng.standard_normal(shape, dtype=np.float32) * np.exp2(rng.integers(-2, 3, shape[:-1] + (1,)))).astype(BF)
        return mx_ref.spread((v.astype(np.float32) * np.exp2(rng.integers(-E, E + 1, shape[:-2] + (1, 1))).astype(np.float32)).astype(BF), rng, e)
    def packed(k):
        c = np.zeros((N, 128, k * 512), np.uint8); s = np.zeros((N, 128, k * 128), np.uint8)
        for r in range(N):
            for i in range(k):
                a, b = mx_ref.quantize(f(128, 512)); c[r][:, 512 * i:512 * i + 512] = a; s[r][:, 128 * i:128 * i + 128] = mx_ref.plane(b, rng)
        return c, s
    d = {}
    d["kc"], d["ks"] = packed(KO)
    d["x"] = f(N, 128, 4 * NC)
    d["wk"] = f(N, 128, G * 512)
    d["q"] = f(N, 128, 512)
    return d
def setup_inputs(rng):
    return inputs(rng, 0, 0)
def setup_inputs_blocks(rng):
    return inputs(rng, 4, 0)
def setup_inputs_wide(rng):
    return inputs(rng, 0, 8)
def reference(kc, ks, x, wk, q):
    new = [mx_ref.quantize(tile(act(layer(wk[r], [mx_ref.quantize(x[r])])))) for r in range(N)]
    y = np.zeros((N, 128, 128 * KO + NC), np.float32)
    for o in range(N):
        old = (np.ascontiguousarray(kc[o]), mx_ref.live(ks[o]))
        qq = mx_ref.quantize(q[o])
        y[o] = np.concatenate([mx_ref.matmul(qq, old), mx_ref.matmul(qq, new[(o - SH) % N])], axis=1)
    return {"y": y}

import numpy as np
from concourse.mybir import dt, AluOpType, ActivationFunctionType

N, SHIFT = 4, 3
C = float(np.float32(0.047))

SCRATCH = {
    "xb": ("sbuf", [128, 512], "bfloat16"),
    "wb": ("sbuf", [128, 1024], "bfloat16"),
    "qb": ("sbuf", [128, 512], "bfloat16"),
    "xc": ("sbuf", [128, 128], "float8_e4m3fn_x4"),
    "xs": ("sbuf", [128, 128], "uint8"),
    "wc": ("sbuf", [128, 256], "float8_e4m3fn_x4"),
    "ws": ("sbuf", [128, 256], "uint8"),
    "qc": ("sbuf", [128, 128], "float8_e4m3fn_x4"),
    "qs": ("sbuf", [128, 128], "uint8"),
    "oldc": ("sbuf", [128, 128], "float8_e4m3fn_x4"),
    "olds": ("sbuf", [128, 128], "uint8"),
    "tile": ("sbuf", [128, 512], "bfloat16"),
    "tc": ("sbuf", [128, 128], "float8_e4m3fn_x4"),
    "ts": ("sbuf", [128, 128], "uint8"),
    "newc": ("sbuf", [128, 128], "float8_e4m3fn_x4"),
    "news": ("sbuf", [128, 128], "uint8"),
    "yo": ("sbuf", [128, 128], "float32"),
    "yn": ("sbuf", [128, 128], "float32"),
    "z": ("psum", [128, 1024], "float32"),
    "s": ("psum", [128, 1024], "float32"),
}
SEMAPHORES = ["ldw", "ldx", "ldq", "ldk", "packed", "z0", "z1", "tiled", "keyed", "qpacked", "s0", "s1", "c0", "c1",
              "sent", "landed", "st0", "st1"]


def rank_program(g, core, T, topo):
    rank = T.rank_of(core)
    if rank is None:
        return
    sem = T.sem
    owner = T.cores[(rank + SHIFT) % N]
    maker = T.cores[(rank - SHIFT) % N]
    mask = topo.mask(core, owner)
    n_out = bin(mask).count("1")
    n_in = bin(topo.mask(maker, core)).count("1")

    g.sync.dma_start(T.wb[:], T.wk[:]).then_inc(sem.ldw, 16)
    g.scalar.dma_start(T.xb[:], T.x[:]).then_inc(sem.ldx, 16)
    g.sync.dma_start(T.qb[:], T.q[:]).then_inc(sem.ldq, 16)
    g.sync.dma_start(T.oldc[:].bitcast(dt.uint8), T.kc[:]).then_inc(sem.ldk, 16)
    g.sync.dma_start(T.olds[:], T.ks[:]).then_inc(sem.ldk, 16)

    g.vector.wait_ge(sem.ldw, 16)
    g.vector.quantize_mx(T.wc[:], T.ws[:], T.wb[:]).then_inc(sem.packed, 1)
    g.vector.wait_ge(sem.ldx, 16)
    g.vector.quantize_mx(T.xc[:], T.xs[:], T.xb[:]).then_inc(sem.packed, 1)
    g.tensor.wait_ge(sem.packed, 2)
    for i in range(2):
        a = 128 * i
        g.tensor.matmul_mx(T.z[:, 512 * i:512 * i + 128], T.wc[:, a:a + 128], T.ws[:, a:a + 128], T.xc[:], T.xs[:],
                           True, True).then_inc(sem["z%d" % i], 1)

    g.scalar.wait_ge(sem.z0, 1)
    for b, c in ((0, C), (1, -C)):
        g.scalar.activation(T.tile[:, b:512:4], T.z[:, 0:128], ActivationFunctionType.Relu, scale=c).then_inc(sem.tiled, 1)
    g.vector.wait_ge(sem.z1, 1)
    for b, c in ((2, C), (3, -C)):
        g.vector.tensor_scalar(T.tile[:, b:512:4], T.z[:, 512:640], c, 0.0, AluOpType.mult, AluOpType.max).then_inc(sem.tiled, 1)
    g.vector.wait_ge(sem.tiled, 4)
    g.vector.quantize_mx(T.tc[:], T.ts[:], T.tile[:]).then_inc(sem.keyed, 1)

    rid, pid = topo.addr(owner, core)
    g.wait_ge(sem.keyed, 1)
    g.remote_dma(T.newc[:].bitcast(dt.uint8), T.tc[:].bitcast(dt.uint8), sem.landed, sem.sent, pid, rid, mask)
    g.remote_dma(T.news[:], T.ts[:], sem.landed, sem.sent, pid, rid, mask)
    g.wait_ge(sem.sent, 2 * n_out)

    g.vector.wait_ge(sem.ldq, 16)
    g.vector.quantize_mx(T.qc[:], T.qs[:], T.qb[:]).then_inc(sem.qpacked, 1)
    g.tensor.wait_ge(sem.qpacked, 1)
    g.tensor.wait_ge(sem.ldk, 32)
    g.tensor.matmul_mx(T.s[:, 0:128], T.qc[:], T.qs[:], T.oldc[:], T.olds[:], True, True).then_inc(sem.s0, 1)
    g.scalar.wait_ge(sem.s0, 1)
    g.scalar.activation(T.yo[:], T.s[:, 0:128], ActivationFunctionType.Copy).then_inc(sem.c0, 1)
    g.scalar.wait_ge(sem.c0, 1)
    g.scalar.dma_start(T.y[:, 0:128], T.yo[:]).then_inc(sem.st0, 16)

    g.tensor.wait_ge(sem.landed, 2 * n_in)
    g.tensor.matmul_mx(T.s[:, 512:640], T.qc[:], T.qs[:], T.newc[:], T.news[:], True, True).then_inc(sem.s1, 1)
    g.vector.wait_ge(sem.s1, 1)
    g.vector.tensor_copy(T.yn[:], T.s[:, 512:640]).then_inc(sem.c1, 1)
    g.sync.wait_ge(sem.c1, 1)
    g.sync.dma_start(T.y[:, 128:256], T.yn[:]).then_inc(sem.st1, 16)
    g.sync.wait_ge(sem.st1, 16)
    g.scalar.wait_ge(sem.st0, 16)
